import numpy as np
import ml_dtypes


def mxq(x, axis, fmt="e4m3"):
    dtype, down = {"e4m3": (ml_dtypes.float8_e4m3fn, 7), "e5m2": (ml_dtypes.float8_e5m2, 14)}[fmt]
    v = np.moveaxis(np.asarray(x, np.float32).astype(ml_dtypes.bfloat16).astype(np.float64), axis, -1)
    blocks = v.reshape(v.shape[:-1] + (-1, 32))
    amax = np.abs(blocks).max(-1, keepdims=True)
    byte = np.maximum(np.where(amax > 0, np.frexp(amax)[1] - 1 + 127, 0) - down, 1)
    scale = np.exp2(byte - 127.0)
    codes = (blocks / scale).astype(np.float32).astype(dtype).astype(np.float64)
    return np.moveaxis((codes * scale).reshape(v.shape), -1, axis)


WIDE = False


def mx_kscale(k):
    if not WIDE:
        return np.ones(k)
    levels = np.array([10, -10, 5, -5, 0])
    if k % 512:
        return np.exp2(np.random.permutation(np.resize(levels, k // 32))).repeat(32)
    a = np.empty((k // 512, 16))
    for p in range(k // 512):
        a[p, :8] = np.random.permutation(np.resize(levels, 8))
        for g in range(8):
            far = levels[np.abs(levels - a[p, g]) >= 10]
            a[p, g + 8] = far[np.random.randint(len(far))]
    return np.exp2(a.ravel()).repeat(32)


def f64(x):
    return np.asarray(x).astype(np.float64)


def striped(idx):
    return np.tile(idx.reshape(-1, 16).T, (8, 1)).astype(np.uint16)


def unstriped(offs):
    return offs[:16].T.reshape(-1).astype(np.int64)


def pack_weight(w):
    k, n = w.shape
    w = f64(np.asarray(w, np.float32).astype(ml_dtypes.bfloat16)).reshape(k // 32, 32, n)
    amax = np.abs(w).max(1)
    byte = np.clip(np.where(amax > 0, np.frexp(amax)[1] - 1 + 127 - 7, 1), 1, 254)
    scaled = (w * np.exp2(127.0 - byte)[:, None, :]).reshape(k, n).astype(np.float32)
    words = np.ascontiguousarray(scaled.reshape(k // 512, 128, 4, n).transpose(0, 1, 3, 2)).astype(ml_dtypes.float8_e4m3fn).view(np.uint8)
    return words, np.ascontiguousarray(byte.astype(np.uint8).reshape(k // 512, 16, n))


def unpack_weight(words, scales):
    g, p, n, _ = words.shape
    vals = np.ascontiguousarray(words).view(ml_dtypes.float8_e4m3fn).astype(np.float64) * np.repeat(np.exp2(scales.astype(np.float64) - 127.0), 8, axis=1)[..., None]
    return vals.transpose(0, 1, 3, 2).reshape(g * 512, n)


K, T, S, D, N = 512, 2048, 1024, 8, 128
P = 2 ** 7


def setup_inputs():
    n = np.random.standard_normal
    s = mx_kscale(K)[:, None]
    packed_xT = pack_weight(n((K, T)) * s)
    return {
        "x_words": packed_xT[0],
        "x_scales": packed_xT[1],
        "w1": (n((K, N)) / np.sqrt(K) / s).astype(np.float32),
        "w2": (n((K, N)) / np.sqrt(K) / s).astype(np.float32),
        "dist": (np.tile(np.random.uniform(0.1, 1.5, S), (P, 1))).astype(np.float32),
        "alb": (np.random.uniform(0.2, 0.9, (N, 1))).astype(np.float32),
        "offs": striped(np.random.permutation(T)[:S]),
    }


def reference(x_words, x_scales, w1, w2, dist, alb, offs):
    xq = unpack_weight(x_words, x_scales)[:, unstriped(offs)]
    ys = mxq(f64(w2), 0, "e4m3").T @ xq
    shp = np.log(np.exp(ys) + 1.0) + 0.3
    sr = shp * f64(dist)[:1]
    prof = shp * ((np.exp(-1.0 * sr) + np.exp(-0.333333 * sr)) / (f64(dist)[:1] + 0.2))
    yi = mxq(f64(w1), 0, "e4m3").T @ xq
    irr = np.exp(0.5 * yi)
    wi = prof * irr
    return np.log(f64(alb) * (wi.reshape(len(wi), -1, D).sum(axis=2)) + 0.1)

@@ -1,0 +1,196 @@
+import math
+from contextlib import ExitStack
+
+import concourse.mybir as mybir
+from concourse.masks import make_identity
+
+K, T, S, D, N = 512, 2048, 1024, 8, 128
+P = 128
+PACK = 4
+FLOPS = 2 * 2 * K * N * S
+
+F32 = mybir.dt.float32
+BF16 = mybir.dt.bfloat16
+I32 = mybir.dt.int32
+U32 = mybir.dt.uint32
+U16 = mybir.dt.uint16
+U8 = mybir.dt.uint8
+FP8X4 = mybir.dt.float8_e4m3fn_x4
+ALU = mybir.AluOpType
+ACT = mybir.ActivationFunctionType
+AX = mybir.AxisListType
+
+CHUNK = 256
+CHUNKS = S // CHUNK
+TILES = S // P
+PER = CHUNK // P
+SLOW = 0.333333
+EXP_CAP = 2.0 ** 60
+
+
+def tile_picked_ybssrd_log_p_kernel(
+    tc, x_words, x_scales, w1, w2, dist, alb, offs, out
+):
+    nc = tc.nc
+    with ExitStack() as ctx:
+        keep = ctx.enter_context(tc.tile_pool(name="keep", bufs=1))
+        psum = ctx.enter_context(tc.psum_pool(name="psum", bufs=1))
+
+        offsets = keep.tile([P, S // 16], U16, name="offsets")
+        nc.sync.dma_start(offsets[:], offs)
+
+        scale_table = keep.tile([P, T], U8, name="scale_table", align_bytes=64)
+        nc.vector.memset(scale_table[:].bitcast(I32), 0)
+        for q in range(4):
+            nc.sync.dma_start(
+                scale_table[32 * q : 32 * q + 4, :].bitcast(I32),
+                x_scales[0, 4 * q : 4 * q + 4, :].bitcast(I32),
+            )
+
+        w2_raw = keep.tile([P, PACK, N], F32, name="w2_raw")
+        nc.sync.dma_start(w2_raw[:], w2.rearrange("(p j) n -> p j n", j=PACK))
+        word_table = keep.tile([P, T], U32, name="word_table", align_bytes=64)
+        nc.sync.dma_start(
+            word_table[:].bitcast(I32),
+            x_words[0].rearrange("p n t -> p (n t)").bitcast(I32),
+        )
+        w1_raw = keep.tile([P, PACK, N], F32, name="w1_raw")
+        nc.sync.dma_start(w1_raw[:], w1.rearrange("(p j) n -> p j n", j=PACK))
+        d = keep.tile([P, TILES], F32, name="d")
+        with nc.allow_non_contiguous_dma(reason="one distance a partition and tile"):
+            nc.sync.dma_start(d[:], dist[0].rearrange("(b p) -> p b", p=P))
+        albedo = keep.tile([P, 1], F32, name="albedo")
+        nc.sync.dma_start(albedo[:], alb)
+
+        ident = keep.tile([P, P], F32, name="ident")
+        make_identity(nc, ident[:])
+
+        def round_weight(raw, name):
+            grouped = keep.tile([P, N, PACK], BF16, name=name, align_bytes=64)
+            nc.scalar.activation(grouped[:], raw[:].rearrange("p j n -> p n j"), ACT.Copy)
+            return grouped
+
+        def quantize_weight(grouped, name):
+            codes = keep.tile([P, N], U32, name=name + "_codes", align_bytes=64)
+            scales = keep.tile([P, N], U8, name=name + "_scales", align_bytes=64)
+            nc.vector.quantize_mx(
+                out=codes[:].bitcast(FP8X4),
+                scales=scales[:],
+                in_=grouped[:].rearrange("p n j -> p (n j)"),
+            )
+            return codes, scales
+
+        w2_bf = round_weight(w2_raw, "w2_bf")
+        x_sc = keep.tile([P, S], U8, name="x_sc", align_bytes=64)
+        nc.vector.tensor_copy(x_sc[:], scale_table[:].indirect(offsets[:]))
+        w2_codes, w2_scales = quantize_weight(w2_bf, "w2")
+        w1_bf = round_weight(w1_raw, "w1_bf")
+
+        x_wd = keep.tile([P, S], U32, name="x_wd", align_bytes=64)
+        banks = [psum.tile([P, 2, CHUNK], F32, name="y%d" % c) for c in range(CHUNKS)]
+
+        def product(b, which, codes, scales):
+            c, h = divmod(b, PER)
+            cols = slice(b * P, (b + 1) * P)
+            nc.tensor.matmul_mx(
+                out=banks[c][:, which, h * P : (h + 1) * P],
+                lhsT=x_wd[:, cols].bitcast(FP8X4),
+                lhsT_scale=x_sc[:, cols],
+                rhs=codes[:].bitcast(FP8X4),
+                rhs_scale=scales[:],
+                start=True,
+                stop=True,
+            )
+
+        e = keep.tile([P, S], F32, name="e")
+        for c in range(CHUNKS):
+            cols = slice(c * CHUNK, (c + 1) * CHUNK)
+            nc.vector.tensor_copy(
+                x_wd[:, cols],
+                word_table[:].indirect(offsets[:, c * CHUNK // 16 : (c + 1) * CHUNK // 16]),
+            )
+            for h in range(PER):
+                product(c * PER + h, 0, w2_codes, w2_scales)
+            nc.scalar.activation(e[:, cols], banks[c][:, 0, :], ACT.Exp)
+
+        w1_codes, w1_scales = quantize_weight(w1_bf, "w1")
+        for b in range(TILES):
+            product(b, 1, w1_codes, w1_scales)
+
+        d_slow = keep.tile([P, TILES], F32, name="d_slow")
+        d_rest = keep.tile([P, TILES], F32, name="d_rest")
+        d_plus = keep.tile([P, TILES], F32, name="d_plus")
+        r = keep.tile([P, TILES], F32, name="r")
+        nc.vector.tensor_scalar(d_plus[:], d[:], 0.2, None, ALU.add)
+        nc.vector.tensor_scalar(d_slow[:], d[:], -2.0 * SLOW, None, ALU.mult)
+        nc.vector.tensor_scalar(d_rest[:], d[:], SLOW - 1.0, None, ALU.mult)
+        nc.vector.reciprocal(r[:], d_plus[:])
+
+        u = keep.tile([P, S], F32, name="u")
+        nc.vector.tensor_scalar(u[:], e[:], EXP_CAP, 1.0, ALU.min, ALU.add)
+
+        lg = keep.tile([P, S], F32, name="lg")
+        shp = keep.tile([P, S], F32, name="shp")
+        arg = keep.tile([P, S], F32, name="arg")
+        for c in range(CHUNKS):
+            cols = slice(c * CHUNK, (c + 1) * CHUNK)
+            nc.scalar.activation(lg[:, cols], u[:, cols], ACT.Ln, scale=math.exp(0.3))
+        for c in range(CHUNKS):
+            cols = slice(c * CHUNK, (c + 1) * CHUNK)
+            nc.vector.scalar_tensor_tensor(
+                shp[:, cols], banks[c][:, 0, :], 0.3, lg[:, cols], ALU.add, ALU.max
+            )
+            for h in range(PER):
+                b = c * PER + h
+                tcols = slice(b * P, (b + 1) * P)
+                nc.vector.scalar_tensor_tensor(
+                    arg[:, tcols], shp[:, tcols], d_slow[:, b : b + 1],
+                    banks[c][:, 1, h * P : (h + 1) * P], ALU.mult, ALU.add,
+                )
+
+        slow = keep.tile([P, S], F32, name="slow")
+        rest = keep.tile([P, S], F32, name="rest")
+        q_t = keep.tile([P, S], F32, name="q_t")
+        wi = keep.tile([P, S], F32, name="wi")
+        sums = keep.tile([P, S // D], F32, name="sums")
+        turned = [psum.tile([P, CHUNK], F32, name="t%d" % c) for c in range(CHUNKS)]
+
+        def group_sum(c):
+            nc.vector.tensor_reduce(
+                sums[:, c * CHUNK // D : (c + 1) * CHUNK // D],
+                turned[c][:].rearrange("p (v d) -> p v d", d=D),
+                AX.X,
+                ALU.add,
+            )
+
+        for c in range(CHUNKS):
+            cols = slice(c * CHUNK, (c + 1) * CHUNK)
+            nc.scalar.activation(slow[:, cols], arg[:, cols], ACT.Exp, scale=0.5)
+            for h in range(PER):
+                b = c * PER + h
+                tcols = slice(b * P, (b + 1) * P)
+                nc.scalar.activation(
+                    rest[:, tcols], shp[:, tcols], ACT.Exp, scale=d_rest[:, b : b + 1]
+                )
+            for h in range(PER):
+                b = c * PER + h
+                tcols = slice(b * P, (b + 1) * P)
+                nc.vector.scalar_tensor_tensor(
+                    q_t[:, tcols], slow[:, tcols], r[:, b : b + 1], shp[:, tcols],
+                    ALU.mult, ALU.mult,
+                )
+            if c > 0:
+                group_sum(c - 1)
+            nc.vector.scalar_tensor_tensor(
+                wi[:, cols], rest[:, cols], 1.0, q_t[:, cols], ALU.add, ALU.mult
+            )
+            for h in range(PER):
+                b = c * PER + h
+                nc.tensor.transpose(
+                    turned[c][:, h * P : (h + 1) * P], wi[:, b * P : (b + 1) * P], ident[:]
+                )
+        group_sum(CHUNKS - 1)
+
+        result = keep.tile([P, S // D], F32, name="result")
+        nc.scalar.activation(result[:], sums[:], ACT.Ln, bias=0.1, scale=albedo[:])
+        nc.sync.dma_start(out, result[:])

@@ -36,39 +36,37 @@ def tile_picked_ybssrd_log_p_kernel(
         keep = ctx.enter_context(tc.tile_pool(name="keep", bufs=1))
         psum = ctx.enter_context(tc.psum_pool(name="psum", bufs=1))
 
+        w2_raw = keep.tile([P, PACK, N], F32, name="w2_raw")
+        nc.sync.dma_start(w2_raw[:], w2.rearrange("(p j) n -> p j n", j=PACK))
         offsets = keep.tile([P, S // 16], U16, name="offsets")
         nc.sync.dma_start(offsets[:], offs)
 
+        d_rows = keep.tile([P, P], F32, name="d_rows")
+        nc.gpsimd.memset(d_rows[:], 0.0)
+        nc.sync.dma_start(d_rows[0:TILES, :], dist[0].rearrange("(b p) -> b p", p=P))
+
         scale_table = keep.tile([P, T], U8, name="scale_table", align_bytes=64)
         nc.vector.memset(scale_table[:].bitcast(I32), 0)
-        for q in range(4):
+        for i in range(4):
             nc.sync.dma_start(
-                scale_table[32 * q : 32 * q + 4, :].bitcast(I32),
-                x_scales[0, 4 * q : 4 * q + 4, :].bitcast(I32),
+                scale_table[i:P:32, :].bitcast(I32),
+                x_scales[0, i:16:4, :].bitcast(I32),
             )
 
-        w2_raw = keep.tile([P, PACK, N], F32, name="w2_raw")
-        nc.sync.dma_start(w2_raw[:], w2.rearrange("(p j) n -> p j n", j=PACK))
-        word_table = keep.tile([P, T], U32, name="word_table", align_bytes=64)
+        word_table = keep.tile([P, T], U32, name="word_table", tag="words", align_bytes=64)
         nc.sync.dma_start(
             word_table[:].bitcast(I32),
             x_words[0].rearrange("p n t -> p (n t)").bitcast(I32),
         )
         w1_raw = keep.tile([P, PACK, N], F32, name="w1_raw")
         nc.sync.dma_start(w1_raw[:], w1.rearrange("(p j) n -> p j n", j=PACK))
-        d = keep.tile([P, TILES], F32, name="d")
-        with nc.allow_non_contiguous_dma(reason="one distance a partition and tile"):
-            nc.sync.dma_start(d[:], dist[0].rearrange("(b p) -> p b", p=P))
-        albedo = keep.tile([P, 1], F32, name="albedo")
-        nc.sync.dma_start(albedo[:], alb)
-
         ident = keep.tile([P, P], F32, name="ident")
         make_identity(nc, ident[:])
-
-        def round_weight(raw, name):
-            grouped = keep.tile([P, N, PACK], BF16, name=name, align_bytes=64)
-            nc.scalar.activation(grouped[:], raw[:].rearrange("p j n -> p n j"), ACT.Copy)
-            return grouped
+        albedo = keep.tile([P, 1], F32, name="albedo")
+        nc.sync.dma_start(albedo[:], alb)
+        d_bank = psum.tile([P, CHUNK], F32, name="d_bank", tag="last_bank")
+        nc.tensor.transpose(d_bank[:, 0:P], d_rows[:], ident[:])
+        d = d_bank[:, 0:TILES]
 
         def quantize_weight(grouped, name):
             codes = keep.tile([P, N], U32, name=name + "_codes", align_bytes=64)
@@ -80,11 +78,11 @@ def tile_picked_ybssrd_log_p_kernel(
             )
             return codes, scales
 
-        w2_bf = round_weight(w2_raw, "w2_bf")
+        w2_bf = keep.tile([P, N, PACK], BF16, name="w2_bf", align_bytes=64)
+        nc.scalar.activation(w2_bf[:], w2_raw[:].rearrange("p j n -> p n j"), ACT.Copy)
+        w2_codes, w2_scales = quantize_weight(w2_bf, "w2")
         x_sc = keep.tile([P, S], U8, name="x_sc", align_bytes=64)
         nc.vector.tensor_copy(x_sc[:], scale_table[:].indirect(offsets[:]))
-        w2_codes, w2_scales = quantize_weight(w2_bf, "w2")
-        w1_bf = round_weight(w1_raw, "w1_bf")
 
         x_wd = keep.tile([P, S], U32, name="x_wd", align_bytes=64)
         banks = [psum.tile([P, 2, CHUNK], F32, name="y%d" % c) for c in range(CHUNKS)]
@@ -102,7 +100,7 @@ def tile_picked_ybssrd_log_p_kernel(
                 stop=True,
             )
 
-        e = keep.tile([P, S], F32, name="e")
+        e = keep.tile([P, S], F32, name="e", tag="exp")
         for c in range(CHUNKS):
             cols = slice(c * CHUNK, (c + 1) * CHUNK)
             nc.vector.tensor_copy(
@@ -113,21 +111,22 @@ def tile_picked_ybssrd_log_p_kernel(
                 product(c * PER + h, 0, w2_codes, w2_scales)
             nc.scalar.activation(e[:, cols], banks[c][:, 0, :], ACT.Exp)
 
+        w1_bf = keep.tile([P, N, PACK], BF16, name="w1_bf", tag="words", align_bytes=64)
+        nc.vector.tensor_copy(w1_bf[:], w1_raw[:].rearrange("p j n -> p n j"))
+
         w1_codes, w1_scales = quantize_weight(w1_bf, "w1")
         for b in range(TILES):
             product(b, 1, w1_codes, w1_scales)
 
-        d_slow = keep.tile([P, TILES], F32, name="d_slow")
-        d_rest = keep.tile([P, TILES], F32, name="d_rest")
-        d_plus = keep.tile([P, TILES], F32, name="d_plus")
-        r = keep.tile([P, TILES], F32, name="r")
-        nc.vector.tensor_scalar(d_plus[:], d[:], 0.2, None, ALU.add)
-        nc.vector.tensor_scalar(d_slow[:], d[:], -2.0 * SLOW, None, ALU.mult)
-        nc.vector.tensor_scalar(d_rest[:], d[:], SLOW - 1.0, None, ALU.mult)
-        nc.vector.reciprocal(r[:], d_plus[:])
-
         u = keep.tile([P, S], F32, name="u")
         nc.vector.tensor_scalar(u[:], e[:], EXP_CAP, 1.0, ALU.min, ALU.add)
+
+        coef = keep.tile([P, 4, TILES], F32, name="coef", tag="exp")
+        d_plus, d_slow, d_rest, r = (coef[:, i, :] for i in range(4))
+        nc.vector.tensor_scalar(d_plus, d, 0.2, None, ALU.add)
+        nc.vector.tensor_scalar(d_slow, d, -2.0 * SLOW, None, ALU.mult)
+        nc.vector.tensor_scalar(d_rest, d, SLOW - 1.0, None, ALU.mult)
+        nc.vector.reciprocal(r, d_plus)
 
         lg = keep.tile([P, S], F32, name="lg")
         shp = keep.tile([P, S], F32, name="shp")
@@ -135,25 +134,64 @@ def tile_picked_ybssrd_log_p_kernel(
         for c in range(CHUNKS):
             cols = slice(c * CHUNK, (c + 1) * CHUNK)
             nc.scalar.activation(lg[:, cols], u[:, cols], ACT.Ln, scale=math.exp(0.3))
-        for c in range(CHUNKS):
-            cols = slice(c * CHUNK, (c + 1) * CHUNK)
+
+        def chunk_cols(c):
+            return slice(c * CHUNK, (c + 1) * CHUNK)
+
+        def tile_cols(b):
+            return slice(b * P, (b + 1) * P)
+
+        def shape(c):
             nc.vector.scalar_tensor_tensor(
-                shp[:, cols], banks[c][:, 0, :], 0.3, lg[:, cols], ALU.add, ALU.max
+                shp[:, chunk_cols(c)], banks[c][:, 0, :], 0.3, lg[:, chunk_cols(c)], ALU.add, ALU.max
             )
+
+        def exponent(c):
             for h in range(PER):
                 b = c * PER + h
-                tcols = slice(b * P, (b + 1) * P)
                 nc.vector.scalar_tensor_tensor(
-                    arg[:, tcols], shp[:, tcols], d_slow[:, b : b + 1],
-                    banks[c][:, 1, h * P : (h + 1) * P], ALU.mult, ALU.add,
+                    arg[:, tile_cols(b)], shp[:, tile_cols(b)], d_slow[:, b : b + 1],
+                    banks[c][:, 1, tile_cols(h)], ALU.mult, ALU.add,
                 )
+
+        shape(0)
+        for c in range(CHUNKS):
+            if c + 1 < CHUNKS:
+                shape(c + 1)
+            exponent(c)
 
         slow = keep.tile([P, S], F32, name="slow")
         rest = keep.tile([P, S], F32, name="rest")
         q_t = keep.tile([P, S], F32, name="q_t")
         wi = keep.tile([P, S], F32, name="wi")
         sums = keep.tile([P, S // D], F32, name="sums")
-        turned = [psum.tile([P, CHUNK], F32, name="t%d" % c) for c in range(CHUNKS)]
+        turned = [psum.tile([P, CHUNK], F32, name="t%d" % c) for c in range(CHUNKS - 1)]
+        turned.append(psum.tile([P, CHUNK], F32, name="t_last", tag="last_bank"))
+
+        def slow_term(c):
+            nc.scalar.activation(slow[:, chunk_cols(c)], arg[:, chunk_cols(c)], ACT.Exp, scale=0.5)
+
+        def rest_term(c):
+            for h in range(PER):
+                b = c * PER + h
+                nc.scalar.activation(
+                    rest[:, tile_cols(b)], shp[:, tile_cols(b)], ACT.Exp, scale=d_rest[:, b : b + 1]
+                )
+
+        def weigh(c):
+            nc.vector.scalar_tensor_tensor(
+                q_t[:, chunk_cols(c)], rest[:, chunk_cols(c)], 1.0, shp[:, chunk_cols(c)],
+                ALU.add, ALU.mult,
+            )
+
+        def finish(c):
+            for h in range(PER):
+                b = c * PER + h
+                nc.vector.scalar_tensor_tensor(
+                    wi[:, tile_cols(b)], slow[:, tile_cols(b)], r[:, b : b + 1],
+                    q_t[:, tile_cols(b)], ALU.mult, ALU.mult,
+                )
+                nc.tensor.transpose(turned[c][:, tile_cols(h)], wi[:, tile_cols(b)], ident[:])
 
         def group_sum(c):
             nc.vector.tensor_reduce(
@@ -164,31 +202,12 @@ def tile_picked_ybssrd_log_p_kernel(
             )
 
         for c in range(CHUNKS):
-            cols = slice(c * CHUNK, (c + 1) * CHUNK)
-            nc.scalar.activation(slow[:, cols], arg[:, cols], ACT.Exp, scale=0.5)
-            for h in range(PER):
-                b = c * PER + h
-                tcols = slice(b * P, (b + 1) * P)
-                nc.scalar.activation(
-                    rest[:, tcols], shp[:, tcols], ACT.Exp, scale=d_rest[:, b : b + 1]
-                )
-            for h in range(PER):
-                b = c * PER + h
-                tcols = slice(b * P, (b + 1) * P)
-                nc.vector.scalar_tensor_tensor(
-                    q_t[:, tcols], slow[:, tcols], r[:, b : b + 1], shp[:, tcols],
-                    ALU.mult, ALU.mult,
-                )
+            rest_term(c)
+            slow_term(c)
+            weigh(c)
             if c > 0:
                 group_sum(c - 1)
-            nc.vector.scalar_tensor_tensor(
-                wi[:, cols], rest[:, cols], 1.0, q_t[:, cols], ALU.add, ALU.mult
-            )
-            for h in range(PER):
-                b = c * PER + h
-                nc.tensor.transpose(
-                    turned[c][:, h * P : (h + 1) * P], wi[:, b * P : (b + 1) * P], ident[:]
-                )
+            finish(c)
         group_sum(CHUNKS - 1)
 
         result = keep.tile([P, S // D], F32, name="result")

@@ -41,10 +41,6 @@ def tile_picked_ybssrd_log_p_kernel(
         offsets = keep.tile([P, S // 16], U16, name="offsets")
         nc.sync.dma_start(offsets[:], offs)
 
-        d_rows = keep.tile([P, P], F32, name="d_rows")
-        nc.gpsimd.memset(d_rows[:], 0.0)
-        nc.sync.dma_start(d_rows[0:TILES, :], dist[0].rearrange("(b p) -> b p", p=P))
-
         scale_table = keep.tile([P, T], U8, name="scale_table", align_bytes=64)
         nc.vector.memset(scale_table[:].bitcast(I32), 0)
         for i in range(4):
@@ -60,11 +56,15 @@ def tile_picked_ybssrd_log_p_kernel(
         )
         w1_raw = keep.tile([P, PACK, N], F32, name="w1_raw")
         nc.sync.dma_start(w1_raw[:], w1.rearrange("(p j) n -> p j n", j=PACK))
+        d_rows = keep.tile([P, P], F32, name="d_rows")
+        nc.vector.memset(d_rows[:], 0.0)
+        nc.sync.dma_start(d_rows[0:TILES, :], dist[0].rearrange("(b p) -> b p", p=P))
         ident = keep.tile([P, P], F32, name="ident")
-        make_identity(nc, ident[:])
+        nc.vector.memset(ident[:], 0.0)
+        make_identity(nc, ident[:], nomemset=True)
         albedo = keep.tile([P, 1], F32, name="albedo")
         nc.sync.dma_start(albedo[:], alb)
-        d_bank = psum.tile([P, CHUNK], F32, name="d_bank", tag="last_bank")
+        d_bank = psum.tile([P, CHUNK], F32, name="d_bank", tag="t2")
         nc.tensor.transpose(d_bank[:, 0:P], d_rows[:], ident[:])
         d = d_bank[:, 0:TILES]
 
@@ -79,16 +79,25 @@ def tile_picked_ybssrd_log_p_kernel(
             return codes, scales
 
         w2_bf = keep.tile([P, N, PACK], BF16, name="w2_bf", align_bytes=64)
-        nc.scalar.activation(w2_bf[:], w2_raw[:].rearrange("p j n -> p n j"), ACT.Copy)
+        w2_view = w2_raw[:].rearrange("p j n -> p n j")
+        nc.scalar.activation(w2_bf[:, : N // 2, :], w2_view[:, : N // 2, :], ACT.Copy)
+        nc.vector.tensor_copy(w2_bf[:, N // 2 :, :], w2_view[:, N // 2 :, :])
         w2_codes, w2_scales = quantize_weight(w2_bf, "w2")
         x_sc = keep.tile([P, S], U8, name="x_sc", align_bytes=64)
         nc.vector.tensor_copy(x_sc[:], scale_table[:].indirect(offsets[:]))
 
         x_wd = keep.tile([P, S], U32, name="x_wd", align_bytes=64)
-        banks = [psum.tile([P, 2, CHUNK], F32, name="y%d" % c) for c in range(CHUNKS)]
+        groups = [(0, 2), (2, 2), (4, 2), (6, 1), (7, 1)]
+        banks = [
+            psum.tile([P, 2, n * P], F32, name="y%d" % g, tag="y%d" % g)
+            for g, (first, n) in enumerate(groups)
+        ]
+        place = {
+            first + h: (g, h) for g, (first, n) in enumerate(groups) for h in range(n)
+        }
 
         def product(b, which, codes, scales):
-            c, h = divmod(b, PER)
+            c, h = place[b]
             cols = slice(b * P, (b + 1) * P)
             nc.tensor.matmul_mx(
                 out=banks[c][:, which, h * P : (h + 1) * P],
@@ -107,9 +116,13 @@ def tile_picked_ybssrd_log_p_kernel(
                 x_wd[:, cols],
                 word_table[:].indirect(offsets[:, c * CHUNK // 16 : (c + 1) * CHUNK // 16]),
             )
-            for h in range(PER):
-                product(c * PER + h, 0, w2_codes, w2_scales)
-            nc.scalar.activation(e[:, cols], banks[c][:, 0, :], ACT.Exp)
+            for g, (first, n) in enumerate(groups):
+                if first // PER == c:
+                    for h in range(n):
+                        product(first + h, 0, w2_codes, w2_scales)
+                    nc.scalar.activation(
+                        e[:, first * P : (first + n) * P], banks[g][:, 0, :], ACT.Exp
+                    )
 
         w1_bf = keep.tile([P, N, PACK], BF16, name="w1_bf", tag="words", align_bytes=64)
         nc.vector.tensor_copy(w1_bf[:], w1_raw[:].rearrange("p j n -> p n j"))
@@ -142,16 +155,19 @@ def tile_picked_ybssrd_log_p_kernel(
             return slice(b * P, (b + 1) * P)
 
         def shape(c):
-            nc.vector.scalar_tensor_tensor(
-                shp[:, chunk_cols(c)], banks[c][:, 0, :], 0.3, lg[:, chunk_cols(c)], ALU.add, ALU.max
-            )
+            for g, (first, n) in enumerate(groups):
+                if first // PER == c:
+                    cols = slice(first * P, (first + n) * P)
+                    nc.vector.scalar_tensor_tensor(
+                        shp[:, cols], banks[g][:, 0, :], 0.3, lg[:, cols], ALU.add, ALU.max
+                    )
 
         def exponent(c):
             for h in range(PER):
                 b = c * PER + h
                 nc.vector.scalar_tensor_tensor(
                     arg[:, tile_cols(b)], shp[:, tile_cols(b)], d_slow[:, b : b + 1],
-                    banks[c][:, 1, tile_cols(h)], ALU.mult, ALU.add,
+                    banks[place[b][0]][:, 1, tile_cols(place[b][1])], ALU.mult, ALU.add,
                 )
 
         shape(0)
@@ -165,8 +181,10 @@ def tile_picked_ybssrd_log_p_kernel(
         q_t = keep.tile([P, S], F32, name="q_t")
         wi = keep.tile([P, S], F32, name="wi")
         sums = keep.tile([P, S // D], F32, name="sums")
-        turned = [psum.tile([P, CHUNK], F32, name="t%d" % c) for c in range(CHUNKS - 1)]
-        turned.append(psum.tile([P, CHUNK], F32, name="t_last", tag="last_bank"))
+        turned = [
+            psum.tile([P, CHUNK], F32, name="turned%d" % c, tag=tag)
+            for c, tag in enumerate(["t0", "t1", "t2", "y0"])
+        ]
 
         def slow_term(c):
             nc.scalar.activation(slow[:, chunk_cols(c)], arg[:, chunk_cols(c)], ACT.Exp, scale=0.5)
@@ -205,9 +223,10 @@ def tile_picked_ybssrd_log_p_kernel(
             rest_term(c)
             slow_term(c)
             weigh(c)
-            if c > 0:
-                group_sum(c - 1)
+            if c >= 2:
+                group_sum(c - 2)
             finish(c)
+        group_sum(CHUNKS - 2)
         group_sum(CHUNKS - 1)
 
         result = keep.tile([P, S // D], F32, name="result")

@@ -219,14 +219,16 @@ def tile_picked_ybssrd_log_p_kernel(
                 ALU.add,
             )
 
-        for c in range(CHUNKS):
-            rest_term(c)
-            slow_term(c)
-            weigh(c)
-            if c >= 2:
-                group_sum(c - 2)
-            finish(c)
-        group_sum(CHUNKS - 2)
+        for step in range(CHUNKS + 3):
+            if step < CHUNKS:
+                rest_term(step)
+            if 2 <= step < CHUNKS + 2 and step >= 3:
+                group_sum(step - 3)
+            if step < CHUNKS:
+                weigh(step)
+            if 1 <= step <= CHUNKS:
+                slow_term(step - 1)
+                finish(step - 1)
         group_sum(CHUNKS - 1)
 
         result = keep.tile([P, S // D], F32, name="result")

import math
from contextlib import ExitStack

import concourse.mybir as mybir
from concourse.masks import make_identity

K, T, S, D, N = 512, 2048, 1024, 8, 128
P = 128
PACK = 4
FLOPS = 2 * 2 * K * N * S

F32 = mybir.dt.float32
BF16 = mybir.dt.bfloat16
I32 = mybir.dt.int32
U32 = mybir.dt.uint32
U16 = mybir.dt.uint16
U8 = mybir.dt.uint8
FP8X4 = mybir.dt.float8_e4m3fn_x4
ALU = mybir.AluOpType
ACT = mybir.ActivationFunctionType
AX = mybir.AxisListType

CHUNK = 256
CHUNKS = S // CHUNK
TILES = S // P
PER = CHUNK // P
SLOW = 0.333333
EXP_CAP = 2.0 ** 60


def tile_picked_ybssrd_log_p_kernel(
    tc, x_words, x_scales, w1, w2, dist, alb, offs, out
):
    nc = tc.nc
    with ExitStack() as ctx:
        keep = ctx.enter_context(tc.tile_pool(name="keep", bufs=1))
        psum = ctx.enter_context(tc.psum_pool(name="psum", bufs=1))

        w2_raw = keep.tile([P, PACK, N], F32, name="w2_raw")
        nc.sync.dma_start(w2_raw[:], w2.rearrange("(p j) n -> p j n", j=PACK))
        offsets = keep.tile([P, S // 16], U16, name="offsets")
        nc.sync.dma_start(offsets[:], offs)

        scale_table = keep.tile([P, T], U8, name="scale_table", align_bytes=64)
        nc.vector.memset(scale_table[:].bitcast(I32), 0)
        for i in range(4):
            nc.sync.dma_start(
                scale_table[i:P:32, :].bitcast(I32),
                x_scales[0, i:16:4, :].bitcast(I32),
            )

        word_table = keep.tile([P, T], U32, name="word_table", tag="words", align_bytes=64)
        nc.sync.dma_start(
            word_table[:].bitcast(I32),
            x_words[0].rearrange("p n t -> p (n t)").bitcast(I32),
        )
        w1_raw = keep.tile([P, PACK, N], F32, name="w1_raw")
        nc.sync.dma_start(w1_raw[:], w1.rearrange("(p j) n -> p j n", j=PACK))
        d_rows = keep.tile([P, P], F32, name="d_rows")
        nc.vector.memset(d_rows[:], 0.0)
        nc.sync.dma_start(d_rows[0:TILES, :], dist[0].rearrange("(b p) -> b p", p=P))
        ident = keep.tile([P, P], F32, name="ident")
        nc.vector.memset(ident[:], 0.0)
        make_identity(nc, ident[:], nomemset=True)
        albedo = keep.tile([P, 1], F32, name="albedo")
        nc.sync.dma_start(albedo[:], alb)
        d_bank = psum.tile([P, CHUNK], F32, name="d_bank", tag="t2")
        nc.tensor.transpose(d_bank[:, 0:P], d_rows[:], ident[:])
        d = d_bank[:, 0:TILES]

        def quantize_weight(grouped, name):
            codes = keep.tile([P, N], U32, name=name + "_codes", align_bytes=64)
            scales = keep.tile([P, N], U8, name=name + "_scales", align_bytes=64)
            nc.vector.quantize_mx(
                out=codes[:].bitcast(FP8X4),
                scales=scales[:],
                in_=grouped[:].rearrange("p n j -> p (n j)"),
            )
            return codes, scales

        w2_bf = keep.tile([P, N, PACK], BF16, name="w2_bf", align_bytes=64)
        w2_view = w2_raw[:].rearrange("p j n -> p n j")
        nc.scalar.activation(w2_bf[:, : N // 2, :], w2_view[:, : N // 2, :], ACT.Copy)
        nc.vector.tensor_copy(w2_bf[:, N // 2 :, :], w2_view[:, N // 2 :, :])
        w2_codes, w2_scales = quantize_weight(w2_bf, "w2")
        x_sc = keep.tile([P, S], U8, name="x_sc", align_bytes=64)
        nc.vector.tensor_copy(x_sc[:], scale_table[:].indirect(offsets[:]))

        x_wd = keep.tile([P, S], U32, name="x_wd", align_bytes=64)
        groups = [(0, 2), (2, 2), (4, 2), (6, 1), (7, 1)]
        banks = [
            psum.tile([P, 2, n * P], F32, name="y%d" % g, tag="y%d" % g)
            for g, (first, n) in enumerate(groups)
        ]
        place = {
            first + h: (g, h) for g, (first, n) in enumerate(groups) for h in range(n)
        }

        def product(b, which, codes, scales):
            c, h = place[b]
            cols = slice(b * P, (b + 1) * P)
            nc.tensor.matmul_mx(
                out=banks[c][:, which, h * P : (h + 1) * P],
                lhsT=x_wd[:, cols].bitcast(FP8X4),
                lhsT_scale=x_sc[:, cols],
                rhs=codes[:].bitcast(FP8X4),
                rhs_scale=scales[:],
                start=True,
                stop=True,
            )

        e = keep.tile([P, S], F32, name="e", tag="exp")
        for c in range(CHUNKS):
            cols = slice(c * CHUNK, (c + 1) * CHUNK)
            nc.vector.tensor_copy(
                x_wd[:, cols],
                word_table[:].indirect(offsets[:, c * CHUNK // 16 : (c + 1) * CHUNK // 16]),
            )
            for g, (first, n) in enumerate(groups):
                if first // PER == c:
                    for h in range(n):
                        product(first + h, 0, w2_codes, w2_scales)
                    nc.scalar.activation(
                        e[:, first * P : (first + n) * P], banks[g][:, 0, :], ACT.Exp
                    )

        w1_bf = keep.tile([P, N, PACK], BF16, name="w1_bf", tag="words", align_bytes=64)
        nc.vector.tensor_copy(w1_bf[:], w1_raw[:].rearrange("p j n -> p n j"))

        w1_codes, w1_scales = quantize_weight(w1_bf, "w1")
        for b in range(TILES):
            product(b, 1, w1_codes, w1_scales)

        u = keep.tile([P, S], F32, name="u")
        nc.vector.tensor_scalar(u[:], e[:], EXP_CAP, 1.0, ALU.min, ALU.add)

        coef = keep.tile([P, 4, TILES], F32, name="coef", tag="exp")
        d_plus, d_slow, d_rest, r = (coef[:, i, :] for i in range(4))
        nc.vector.tensor_scalar(d_plus, d, 0.2, None, ALU.add)
        nc.vector.tensor_scalar(d_slow, d, -2.0 * SLOW, None, ALU.mult)
        nc.vector.tensor_scalar(d_rest, d, SLOW - 1.0, None, ALU.mult)
        nc.vector.reciprocal(r, d_plus)

        lg = keep.tile([P, S], F32, name="lg")
        shp = keep.tile([P, S], F32, name="shp")
        arg = keep.tile([P, S], F32, name="arg")
        for c in range(CHUNKS):
            cols = slice(c * CHUNK, (c + 1) * CHUNK)
            nc.scalar.activation(lg[:, cols], u[:, cols], ACT.Ln, scale=math.exp(0.3))

        def chunk_cols(c):
            return slice(c * CHUNK, (c + 1) * CHUNK)

        def tile_cols(b):
            return slice(b * P, (b + 1) * P)

        def shape(c):
            for g, (first, n) in enumerate(groups):
                if first // PER == c:
                    cols = slice(first * P, (first + n) * P)
                    nc.vector.scalar_tensor_tensor(
                        shp[:, cols], banks[g][:, 0, :], 0.3, lg[:, cols], ALU.add, ALU.max
                    )

        def exponent(c):
            for h in range(PER):
                b = c * PER + h
                nc.vector.scalar_tensor_tensor(
                    arg[:, tile_cols(b)], shp[:, tile_cols(b)], d_slow[:, b : b + 1],
                    banks[place[b][0]][:, 1, tile_cols(place[b][1])], ALU.mult, ALU.add,
                )

        shape(0)
        for c in range(CHUNKS):
            if c + 1 < CHUNKS:
                shape(c + 1)
            exponent(c)

        slow = keep.tile([P, S], F32, name="slow")
        rest = keep.tile([P, S], F32, name="rest")
        q_t = keep.tile([P, S], F32, name="q_t")
        wi = keep.tile([P, S], F32, name="wi")
        sums = keep.tile([P, S // D], F32, name="sums")
        turned = [
            psum.tile([P, CHUNK], F32, name="turned%d" % c, tag=tag)
            for c, tag in enumerate(["t0", "t1", "t2", "y0"])
        ]

        def slow_term(c):
            nc.scalar.activation(slow[:, chunk_cols(c)], arg[:, chunk_cols(c)], ACT.Exp, scale=0.5)

        def rest_term(c):
            for h in range(PER):
                b = c * PER + h
                nc.scalar.activation(
                    rest[:, tile_cols(b)], shp[:, tile_cols(b)], ACT.Exp, scale=d_rest[:, b : b + 1]
                )

        def weigh(c):
            nc.vector.scalar_tensor_tensor(
                q_t[:, chunk_cols(c)], rest[:, chunk_cols(c)], 1.0, shp[:, chunk_cols(c)],
                ALU.add, ALU.mult,
            )

        def finish(c):
            for h in range(PER):
                b = c * PER + h
                nc.vector.scalar_tensor_tensor(
                    wi[:, tile_cols(b)], slow[:, tile_cols(b)], r[:, b : b + 1],
                    q_t[:, tile_cols(b)], ALU.mult, ALU.mult,
                )
                nc.tensor.transpose(turned[c][:, tile_cols(h)], wi[:, tile_cols(b)], ident[:])

        def group_sum(c):
            nc.vector.tensor_reduce(
                sums[:, c * CHUNK // D : (c + 1) * CHUNK // D],
                turned[c][:].rearrange("p (v d) -> p v d", d=D),
                AX.X,
                ALU.add,
            )

        for step in range(CHUNKS + 3):
            if step < CHUNKS:
                rest_term(step)
            if 2 <= step < CHUNKS + 2 and step >= 3:
                group_sum(step - 3)
            if step < CHUNKS:
                weigh(step)
            if 1 <= step <= CHUNKS:
                slow_term(step - 1)
                finish(step - 1)
        group_sum(CHUNKS - 1)

        result = keep.tile([P, S // D], F32, name="result")
        nc.scalar.activation(result[:], sums[:], ACT.Ln, bias=0.1, scale=albedo[:])
        nc.sync.dma_start(out, result[:])
